import numpy as np
import ml_dtypes


def mxq(x, axis, fmt="e4m3"):
    dtype, down = {"e4m3": (ml_dtypes.float8_e4m3fn, 7), "e5m2": (ml_dtypes.float8_e5m2, 14)}[fmt]
    v = np.moveaxis(np.asarray(x, np.float32).astype(ml_dtypes.bfloat16).astype(np.float64), axis, -1)
    blocks = v.reshape(v.shape[:-1] + (-1, 32))
    amax = np.abs(blocks).max(-1, keepdims=True)
    byte = np.maximum(np.where(amax > 0, np.frexp(amax)[1] - 1 + 127, 0) - down, 1)
    scale = np.exp2(byte - 127.0)
    codes = (blocks / scale).astype(np.float32).astype(dtype).astype(np.float64)
    return np.moveaxis((codes * scale).reshape(v.shape), -1, axis)


WIDE = False


def mx_kscale(k):
    if not WIDE:
        return np.ones(k)
    levels = np.array([10, -10, 5, -5, 0])
    if k % 512:
        return np.exp2(np.random.permutation(np.resize(levels, k // 32))).repeat(32)
    a = np.empty((k // 512, 16))
    for p in range(k // 512):
        a[p, :8] = np.random.permutation(np.resize(levels, 8))
        for g in range(8):
            far = levels[np.abs(levels - a[p, g]) >= 10]
            a[p, g + 8] = far[np.random.randint(len(far))]
    return np.exp2(a.ravel()).repeat(32)


BF16 = ml_dtypes.bfloat16


def bf(x):
    return np.asarray(x, np.float32).astype(BF16)


def f64(x):
    return np.asarray(x).astype(np.float64)


E2M1 = np.array([0.0, 0.5, 1.0, 1.5, 2.0, 3.0, 4.0, 6.0, -0.0, -0.5, -1.0, -1.5, -2.0, -3.0, -4.0, -6.0])


def pack_weight(w, fmt):
    k, n = w.shape
    w = f64(bf(w)).reshape(k // 32, 32, n)
    amax = np.abs(w).max(1)
    if fmt == "e4m3":
        byte = np.frexp(amax)[1] - 1 + 127 - 7
    else:
        mant, ex = np.frexp(amax / 6.0)
        byte = np.where(mant > 0.5, ex, ex - 1) + 127
    byte = np.clip(np.where(amax > 0, byte, 1), 1, 254)
    scaled = (w * np.exp2(127.0 - byte)[:, None, :]).reshape(k, n).astype(np.float32)
    by_word = np.ascontiguousarray(scaled.reshape(k // 512, 128, 4, n).transpose(0, 1, 3, 2))
    if fmt == "e4m3":
        words = by_word.astype(ml_dtypes.float8_e4m3fn).view(np.uint8)
    else:
        c = by_word.astype(ml_dtypes.float4_e2m1fn).view(np.uint8) & 0xF
        words = c[..., 0::2] | (c[..., 1::2] << 4)
    return np.ascontiguousarray(words), np.ascontiguousarray(byte.astype(np.uint8).reshape(k // 512, 16, n))


def unpack_weight(words, scales, fmt):
    g, p, n, _ = words.shape
    if fmt == "e4m3":
        vals = np.ascontiguousarray(words).view(ml_dtypes.float8_e4m3fn).astype(np.float64)
    else:
        nib = np.empty((g, p, n, 4), np.uint8)
        nib[..., 0::2] = words & 0xF
        nib[..., 1::2] = words >> 4
        vals = E2M1[nib]
    vals = vals * np.repeat(np.exp2(scales.astype(np.float64) - 127.0), 8, axis=1)[..., None]
    return vals.transpose(0, 1, 3, 2).reshape(g * 512, n)
def pack4(w):
    words, scales = pack_weight(w, "e2m1")
    return words.reshape(words.shape[0], 128, -1), scales


def unpack4(words, scales):
    return unpack_weight(words.reshape(words.shape[0], 128, -1, 2), scales, "e2m1")


I, J, C, K, R = 1024, 1024, 2, 1024, 512


def draw0():
    s = mx_kscale(K)
    t = mx_kscale(C * J)
    u = mx_kscale(I)
    left = np.random.standard_normal((I, K)) * s * u[:, None]
    right = np.random.standard_normal((C * J, K)) / np.sqrt(K) / s * t[:, None]
    prior = 0.5 * np.random.standard_normal((I, C * J)) * u[:, None] * t
    near = np.random.uniform(0.2, 1.8, (I, J))
    v = np.random.standard_normal((C * J, R)) / np.sqrt(C * J) / t[:, None]
    y = np.random.standard_normal((I, R)) / np.sqrt(I) / u[:, None]
    v_words, v_scales = pack4(v)
    return {"left": bf(left), "right": bf(right), "prior": bf(prior), "near": bf(near),
            "v_words": v_words, "v_scales": v_scales, "y": bf(y)}


def core(left, right, prior, near, v_words, v_scales, y):
    z = mxq(f64(left), 1, "e4m3") @ mxq(f64(right), 1, "e4m3").T
    z = np.maximum(z + f64(prior), 0.0)
    z = (z.reshape(I, C, J) * f64(near)[:, None, :]).reshape(I, C * J)
    to_ligand = mxq(z, 1, "e4m3") @ unpack4(v_words, v_scales)
    to_receptor = mxq(z, 0, "e4m3").T @ mxq(f64(y), 0, "e4m3")
    return to_ligand, to_receptor


def e4m3fn_bytes(y):
    return np.clip(np.asarray(y, np.float64), -448.0, 448.0).astype(np.float32).astype(ml_dtypes.float8_e4m3fn).view(np.uint8)


def e4m3fn_values(b):
    return np.asarray(b, np.uint8).view(ml_dtypes.float8_e4m3fn).astype(np.float64)


def setup_inputs():
    d = draw0()
    x0 = np.asarray(d['y']).astype(np.float64)
    s = (np.max(np.abs(x0), axis=(1,), keepdims=True) / 448.0).astype(np.float32)
    out = {}
    for k, v in d.items():
        if k == 'y':
            out['y_bytes'] = e4m3fn_bytes(x0 / s.astype(np.float64))
            out['y_scale'] = s
        else:
            out[k] = v
    return out


def reference(left, right, prior, near, v_words, v_scales, y_bytes, y_scale):
    return core(left, right, prior, near, v_words, v_scales, e4m3fn_values(y_bytes) * y_scale.astype(np.float64))

@@ -1,0 +1,458 @@
+from contextlib import ExitStack
+
+import concourse.mybir as mybir
+from concourse.masks import make_identity
+
+I, J, C, K, R = 1024, 1024, 2, 1024, 512
+M = C * J
+FLOPS = 2 * I * M * K + 2 * I * M * R + 2 * I * M * R
+
+F32 = mybir.dt.float32
+BF16 = mybir.dt.bfloat16
+I32 = mybir.dt.int32
+U32 = mybir.dt.uint32
+U8 = mybir.dt.uint8
+FP8 = mybir.dt.float8_e4m3fn
+FP8X4 = mybir.dt.float8_e4m3fn_x4
+FP4X4 = mybir.dt.float4_e2m1fn_x4
+ADD = mybir.AluOpType.add
+MAX = mybir.AluOpType.max
+MULT = mybir.AluOpType.mult
+COPY = mybir.ActivationFunctionType.Copy
+
+P = 128
+ORDER = [(0, 0), (1, 0), (0, 1), (1, 1), (0, 2), (0, 3), (1, 2), (1, 3)]
+N_UNITS = len(ORDER)
+
+
+def tile_pair_tensor_messages_s8_kernel(
+    tc, left, right, prior, near, v_words, v_scales, y_bytes, y_scale, to_ligand, to_receptor
+):
+    nc = tc.nc
+    left_v = left.rearrange("(g p t) d -> g p t d", p=P, t=4)
+    right_v = right.rearrange("(g p t) d -> g p t d", p=P, t=4)
+    prior_v = prior.rearrange("(g p t) m -> g p t m", p=P, t=4)
+    near_v = near.rearrange("(g p t) m -> g p t m", p=P, t=4)
+    lig_v = to_ligand.rearrange("(g p t) r -> g t p r", p=P, t=4)
+    rec_v = to_receptor.rearrange("(g p t) r -> g t p r", p=P, t=4)
+
+    with ExitStack() as ctx:
+        keep = ctx.enter_context(tc.tile_pool(name="keep", bufs=1))
+        work = ctx.enter_context(tc.tile_pool(name="work", bufs=2))
+        s1_pool = ctx.enter_context(tc.psum_pool(name="s1", bufs=1))
+        w_pool = ctx.enter_context(tc.psum_pool(name="w", bufs=4))
+        ctx.enter_context(tc.manual_schedule())
+
+        ident = keep.tile([P, P], F32, name="ident", align_bytes=64)
+        make_identity(nc, ident[:])
+        warm = keep.tile([P, 2], F32, name="warm", align_bytes=64)
+        nc.gpsimd.memset(warm[:], 0.0)
+        v_tile = keep.tile([P, 4, 2 * R], U8, name="v_tile", align_bytes=64)
+        vs_tile = keep.tile([P, 4, R], U8, name="vs_tile", align_bytes=64)
+        nc.gpsimd.memset(vs_tile[:].rearrange("p g n -> p (g n)").bitcast(I32), 0)
+        nc.scalar.activation(warm[:, 1:2], warm[:, 0:1], COPY)
+
+        lc = [keep.tile([P, 4, 2, P], U32, name=f"lc{g}", align_bytes=64) for g in range(2)]
+        ls = [keep.tile([P, 4, 2, P], U8, name=f"ls{g}", align_bytes=64) for g in range(2)]
+        rc = [keep.tile([P, 2, 4 * P], U32, name=f"rc{g}", align_bytes=64) for g in range(4)]
+        rs = [keep.tile([P, 2, 4 * P], U8, name=f"rs{g}", align_bytes=64) for g in range(4)]
+        yc = [keep.tile([P, R], U32, name=f"yc{g}", align_bytes=64) for g in range(2)]
+        ys = [keep.tile([P, R], U8, name=f"ys{g}", align_bytes=64) for g in range(2)]
+        za_c, za_s, zb_c, zb_s = {}, {}, {}, {}
+        for g, b in ORDER:
+            za_c[g, b] = keep.tile([P, 4 * P], U32, name=f"zac{g}{b}", align_bytes=64)
+            za_s[g, b] = keep.tile([P, 4 * P], U8, name=f"zas{g}{b}", align_bytes=64)
+            zb_c[g, b] = keep.tile([P, 4, P], U32, name=f"zbc{g}{b}", align_bytes=64)
+            zb_s[g, b] = keep.tile([P, 4, P], U8, name=f"zbs{g}{b}", align_bytes=64)
+
+        raws, priors, nears = {}, {}, {}
+
+        def raw_tile(key):
+            raw = work.tile([P, 4, K], BF16, name="raw", tag="raw", bufs=4, align_bytes=64)
+            raws[key] = raw
+
+        def load_raw(key, t0, t1):
+            side, g = key
+            view = left_v if side == "l" else right_v
+            nc.sync.dma_start(out=raws[key][:, t0:t1, :], in_=view[g, :, t0:t1, :])
+
+        def load_prior(g, b):
+            t = work.tile([P, 4, 4 * P], BF16, name="prior_t", tag="prior_t", bufs=5, align_bytes=64)
+            nc.sync.dma_start(out=t[:], in_=prior_v[g, :, :, 512 * b : 512 * (b + 1)])
+            priors[g, b] = t
+
+        def load_near(g, b):
+            t = keep.tile([P, 4, 4 * P], BF16, name=f"near{g}{b}", align_bytes=64)
+            nc.sync.dma_start(out=t[:], in_=near_v[g, :, :, 512 * b : 512 * (b + 1)])
+            nears[g, b] = t
+
+        def transpose_rows(key, t):
+            words = raws[key][:].rearrange("p t d -> p (t d)").bitcast(F32)
+            bank = w_pool.tile([P, 2, 2, P], F32, name="bank", tag="bank", bufs=4)
+            for h in range(2):
+                for u in range(2):
+                    lo = 512 * t + 256 * h
+                    nc.tensor.transpose(bank[:, h, u, :], words[:, lo + u : lo + 256 : 2], ident[:])
+            return bank
+
+        grouped = {}
+
+        def copy_rows(key, t, bank, on_vector):
+            side, g = key
+            src = bank[:].rearrange("x h u p -> x h p u")
+            if side == "l":
+                if t == 0:
+                    grouped[key] = work.tile([P, 4, 2, P, 4], BF16, name="rin", tag="rin", bufs=3, align_bytes=64)
+                dst = grouped[key][:, t].rearrange("x h p e -> x (h p e)").bitcast(F32)
+                dst = dst.rearrange("x (h p u) -> x h p u", h=2, u=2)
+            else:
+                if t == 0:
+                    grouped[key] = work.tile([P, 2, 4, P, 4], BF16, name="rin", tag="rin", bufs=3, align_bytes=64)
+                dst = grouped[key][:].rearrange("x h s p e -> x (h s p e)").bitcast(F32)
+                dst = dst.rearrange("x (h s p u) -> x h s p u", h=2, s=4, u=2)[:, :, t]
+            if on_vector:
+                nc.vector.tensor_copy(out=dst, in_=src)
+            else:
+                nc.scalar.copy(out=dst, in_=src)
+
+        def quantize_left(g, t0, t1):
+            nc.vector.quantize_mx(
+                out=lc[g][:, t0:t1].rearrange("x t h p -> x (t h p)").bitcast(FP8X4),
+                scales=ls[g][:, t0:t1].rearrange("x t h p -> x (t h p)"),
+                in_=grouped["l", g][:, t0:t1].rearrange("x t h p e -> x (t h p e)"),
+            )
+
+        def quantize_right(g, h, s0=0, s1=4):
+            nc.vector.quantize_mx(
+                out=rc[g][:, h, P * s0 : P * s1].bitcast(FP8X4),
+                scales=rs[g][:, h, P * s0 : P * s1],
+                in_=grouped["r", g][:, h, s0:s1].rearrange("x s p e -> x (s p e)"),
+            )
+
+        s1_banks = {}
+
+        def stage1(k, t):
+            g, b = ORDER[k]
+            bank = s1_pool.tile([P, 4 * P], F32, name="s1b", tag=f"s1b{t}", bufs=1)
+            for h in range(2):
+                nc.tensor.matmul_mx(
+                    out=bank[:],
+                    lhsT=lc[g][:, t, h, :].bitcast(FP8X4),
+                    lhsT_scale=ls[g][:, t, h, :],
+                    rhs=rc[b][:, h, :].bitcast(FP8X4),
+                    rhs_scale=rs[b][:, h, :],
+                    start=(h == 0),
+                    stop=(h == 1),
+                )
+            s1_banks[k, t] = bank
+
+        sums, zis, lis = {}, {}, {}
+
+        def add_prior(k, t):
+            g, b = ORDER[k]
+            if t == 0:
+                sums[k] = work.tile([P, 4, 4 * P], F32, name="sum_t", tag="sum_t", bufs=2, align_bytes=64)
+            nc.vector.tensor_tensor(
+                out=sums[k][:, t, :].rearrange("p (s q) -> p s q", s=4),
+                in0=s1_banks[k, t][:].rearrange("p (s q) -> p s q", s=4),
+                in1=priors[g, b][:, t, :].rearrange("p (q s) -> p s q", s=4),
+                op=ADD,
+            )
+
+        def relu_near(k, s):
+            g, b = ORDER[k]
+            if s == 0:
+                zis[k] = work.tile([P, 4 * P, 4], BF16, name="zi", tag="zi", bufs=3, align_bytes=64)
+            nc.vector.scalar_tensor_tensor(
+                out=zis[k][:, P * s : P * (s + 1), :],
+                in0=sums[k][:, :, P * s : P * (s + 1)].rearrange("p t q -> p q t"),
+                scalar=0.0,
+                in1=nears[g, b % 2][:].rearrange("p t (q s) -> p s q t", s=4)[:, s],
+                op0=MAX,
+                op1=MULT,
+            )
+
+        def quantize_a(k, s0=0, s1=4):
+            g, b = ORDER[k]
+            nc.vector.quantize_mx(
+                out=za_c[g, b][:, P * s0 : P * s1].bitcast(FP8X4),
+                scales=za_s[g, b][:, P * s0 : P * s1],
+                in_=zis[k][:, P * s0 : P * s1].rearrange("p m t -> p (m t)"),
+            )
+
+        z_banks = {}
+
+        def transpose_z(k, u, s0=0, s1=4):
+            words = zis[k][:].rearrange("p m t -> p (m t)").bitcast(F32)
+            if s0 == 0:
+                z_banks[k, u] = w_pool.tile([P, 4, P], F32, name="bank", tag="bank", bufs=4)
+            for s in range(s0, s1):
+                nc.tensor.transpose(z_banks[k, u][:, s, :], words[:, 256 * s + u : 256 * (s + 1) : 2], ident[:])
+
+        def copy_b(k, u, on_vector=False):
+            if u == 0:
+                lis[k] = work.tile([P, 2, 2, P, 4], BF16, name="li", tag="li", bufs=2, align_bytes=64)
+            dst = lis[k][:, u]
+            src = z_banks[k, u][:].rearrange("q s p -> q (s p)").bitcast(BF16).rearrange("q (s p e) -> q e p s", s=4, e=2)
+            if on_vector:
+                nc.vector.tensor_copy(out=dst, in_=src)
+            else:
+                nc.scalar.copy(out=dst, in_=src)
+
+        def quantize_b(k, u0=0, u1=2):
+            g, b = ORDER[k]
+            nc.vector.quantize_mx(
+                out=zb_c[g, b][:, 2 * u0 : 2 * u1].rearrange("q t p -> q (t p)").bitcast(FP8X4),
+                scales=zb_s[g, b][:, 2 * u0 : 2 * u1].rearrange("q t p -> q (t p)"),
+                in_=lis[k][:, u0:u1].rearrange("q u e p s -> q (u e p s)"),
+            )
+
+        outs = {}
+
+        def finish(bank, kind, g, t, on_vector):
+            if (kind, g) not in outs:
+                outs[kind, g] = work.tile([P, 4, R], F32, name="raw", tag="raw", bufs=4, align_bytes=64)
+            o = outs[kind, g][:, t, :]
+            if on_vector:
+                nc.vector.tensor_copy(out=o, in_=bank[:])
+            else:
+                nc.scalar.copy(out=o, in_=bank[:])
+            nc.sync.dma_start(out=(rec_v if kind == "r" else lig_v)[g, t], in_=o)
+
+        def receptor(b, s, on_vector=False):
+            bank = w_pool.tile([P, R], F32, name="bank", tag="bank", bufs=4)
+            for g in range(2):
+                nc.tensor.matmul_mx(
+                    out=bank[:],
+                    lhsT=za_c[g, b][:, P * s : P * (s + 1)].bitcast(FP8X4),
+                    lhsT_scale=za_s[g, b][:, P * s : P * (s + 1)],
+                    rhs=yc[g][:].bitcast(FP8X4),
+                    rhs_scale=ys[g][:],
+                    start=(g == 0),
+                    stop=(g == 1),
+                )
+            finish(bank, "r", b, s, on_vector)
+
+        def ligand_passes(bank, g, t, blocks):
+            for b in blocks:
+                nc.tensor.matmul_mx(
+                    out=bank[:],
+                    lhsT=zb_c[g, b][:, t, :].bitcast(FP8X4),
+                    lhsT_scale=zb_s[g, b][:, t, :],
+                    rhs=v_tile[:, b, :].bitcast(FP4X4),
+                    rhs_scale=vs_tile[:, b, :],
+                    start=(b == 0),
+                    stop=(b == 3),
+                )
+
+        def ligand(g, t, on_vector=False):
+            bank = w_pool.tile([P, R], F32, name="bank", tag="bank", bufs=4)
+            ligand_passes(bank, g, t, range(4))
+            finish(bank, "l", g, t, on_vector)
+
+        y_codes = keep.tile([P, 2, 4, R], U8, name="y_codes", align_bytes=64)
+        y_sc = keep.tile([P, 2, 4], F32, name="y_sc", align_bytes=64)
+        y_plane, y_group = {}, {}
+
+        def load_y():
+            nc.sync.dma_start(out=y_sc[:], in_=y_scale.rearrange("(g p t) o -> p g (t o)", p=P, t=4))
+            nc.sync.dma_start(out=y_codes[:], in_=y_bytes.rearrange("(g p t) r -> p g t r", p=P, t=4))
+
+        def widen_y(g):
+            y_plane[g] = work.tile([P, 4, R], BF16, name="y_plane", tag="y_plane", bufs=2, align_bytes=64)
+            for t in range(4):
+                nc.scalar.activation(
+                    y_plane[g][:, t, :], y_codes[:, g, t, :].bitcast(FP8), COPY, scale=y_sc[:, g, t : t + 1]
+                )
+
+        def group_y(g):
+            y_group[g] = work.tile([P, R, 4], BF16, name="y_group", tag="y_group", bufs=1, align_bytes=64)
+            nc.vector.tensor_copy(
+                out=y_group[g][:].rearrange("p (c i) t -> p c t i", i=4),
+                in_=y_plane[g][:].rearrange("p t (c i) -> p c t i", i=4),
+            )
+
+        def quantize_y(g):
+            nc.vector.quantize_mx(
+                out=yc[g][:].bitcast(FP8X4), scales=ys[g][:], in_=y_group[g][:].rearrange("p r t -> p (r t)")
+            )
+
+        L0, R0, L1, R1, R2, R3 = ("l", 0), ("r", 0), ("l", 1), ("r", 1), ("r", 2), ("r", 3)
+        for key in (L0, R0, L1, R1):
+            raw_tile(key)
+        load_raw(L0, 0, 1)
+        for s in range(4):
+            load_raw(R0, s, s + 1)
+        load_raw(L0, 1, 2)
+        load_raw(L0, 2, 4)
+        load_prior(0, 0)
+        load_y()
+        load_raw(L1, 0, 2)
+        load_near(0, 0)
+        load_raw(L1, 2, 4)
+        load_prior(1, 0)
+        load_near(1, 0)
+        load_raw(R1, 0, 2)
+        load_raw(R1, 2, 4)
+        load_prior(0, 1)
+        load_near(0, 1)
+        load_prior(1, 1)
+        load_near(1, 1)
+
+        def rows(key, t, on_vector=False):
+            bank = transpose_rows(key, t)
+            copy_rows(key, t, bank, on_vector)
+
+        rows(L0, 0, True)
+        rows(R0, 0)
+        rows(R0, 1, True)
+        quantize_left(0, 0, 1)
+        quantize_right(0, 0, 0, 1)
+        quantize_right(0, 1, 0, 1)
+        rows(R0, 2)
+        rows(R0, 3, True)
+        quantize_right(0, 0, 1, 3)
+        quantize_right(0, 1, 1, 3)
+        quantize_right(0, 0, 3, 4)
+        quantize_right(0, 1, 3, 4)
+        rows(L0, 1)
+        stage1(0, 0)
+        quantize_left(0, 1, 2)
+        rows(L0, 2)
+        rows(L0, 3)
+        stage1(0, 1)
+        add_prior(0, 0)
+        quantize_left(0, 2, 4)
+        stage1(0, 2)
+        stage1(0, 3)
+        for t in range(1, 4):
+            add_prior(0, t)
+        widen_y(0)
+        for t in range(4):
+            rows(L1, t)
+        relu_near(0, 0)
+        relu_near(0, 1)
+        quantize_left(1, 0, 2)
+        relu_near(0, 2)
+        quantize_left(1, 2, 4)
+        for t in range(4):
+            stage1(1, t)
+        relu_near(0, 3)
+        group_y(0)
+        widen_y(1)
+        for t in range(4):
+            rows(R1, t)
+
+        raw_tile(R2)
+        load_raw(R2, 0, 4)
+        load_prior(0, 2)
+        raw_tile(R3)
+        load_raw(R3, 0, 4)
+
+        def load_v():
+            nc.sync.dma_start(
+                out=v_tile[:].rearrange("p g n -> p (g n)").bitcast(I32).rearrange("p (g n) -> p g n", g=4),
+                in_=v_words.bitcast(I32).rearrange("g p n -> p g n"),
+            )
+            vs_words = vs_tile[:].rearrange("p g n -> p (g n)").bitcast(I32).rearrange("p (g n) -> p g n", g=4)
+            for quad in range(4):
+                nc.sync.dma_start(
+                    out=vs_words[32 * quad : 32 * quad + 4],
+                    in_=v_scales.bitcast(I32)[:, 4 * quad : 4 * quad + 4, :].rearrange("g q n -> q g n"),
+                )
+
+        lig_banks = {}
+
+        def ligand_open(g, t, pool_tag):
+            if pool_tag:
+                lig_banks[g, t] = s1_pool.tile([P, R], F32, name="s1b", tag=f"s1b{t}", bufs=1)
+            else:
+                lig_banks[g, t] = w_pool.tile([P, R], F32, name="bank", tag="bank", bufs=4)
+            ligand_passes(lig_banks[g, t], g, t, range(2 if pool_tag else 3))
+
+        def ligand_close(g, t, on_vector=False):
+            ligand_passes(lig_banks[g, t], g, t, range(3, 4))
+            finish(lig_banks[g, t], "l", g, t, on_vector)
+
+        last = N_UNITS - 1
+        ahead = {1: R2, 2: R3}
+        fresh = {1: R1, 3: R2, 4: R3}
+        for k in range(1, N_UNITS):
+            for t in range(4):
+                add_prior(k, t)
+            for u in range(2):
+                transpose_z(k - 1, u)
+                copy_b(k - 1, u)
+            if k == 1:
+                load_v()
+                load_prior(0, 3)
+                load_prior(1, 2)
+            if k == 2:
+                load_prior(1, 3)
+            key = fresh.get(k)
+            if key is not None:
+                quantize_right(key[1], 0)
+                quantize_right(key[1], 1)
+            if k < last:
+                for t in range(4):
+                    stage1(k + 1, t)
+            quantize_a(k - 1)
+            relu_near(k, 0)
+            relu_near(k, 1)
+            if k == 1:
+                quantize_y(0)
+                group_y(1)
+            if k == 2:
+                quantize_y(1)
+            key = ahead.get(k)
+            if key is not None:
+                for t in range(4):
+                    rows(key, t)
+            if k == 3:
+                receptor(0, 0)
+                receptor(0, 1)
+                receptor(0, 2)
+                receptor(0, 3)
+            if k == 4:
+                for s in range(4):
+                    receptor(1, s)
+            quantize_b(k - 1)
+            if k == 5:
+                ligand_open(0, 0, False)
+                ligand_open(0, 1, False)
+            if k == 6:
+                ligand_close(0, 0)
+                ligand_close(0, 1)
+                ligand(0, 2)
+                ligand(0, 3)
+            if k < last:
+                relu_near(k, 2)
+                relu_near(k, 3)
+
+        for t in range(4):
+            ligand_open(1, t, True)
+        for s in range(3):
+            receptor(2, s)
+        quantize_a(last, 0, 2)
+        relu_near(last, 2)
+        relu_near(last, 3)
+        for u in range(2):
+            transpose_z(last, u, 0, 2)
+        receptor(2, 3)
+        receptor(3, 0)
+        for u in range(2):
+            transpose_z(last, u, 2, 4)
+        for t in range(4):
+            ligand_passes(lig_banks[1, t], 1, t, [2])
+        copy_b(last, 0)
+        copy_b(last, 1, True)
+        quantize_a(last, 2, 4)
+        quantize_b(last, 0, 1)
+        quantize_b(last, 1, 2)
+        receptor(3, 1)
+        receptor(3, 2, True)
+        ligand_close(1, 0)
+        ligand_close(1, 1, True)
+        ligand_close(1, 2)
+        ligand_close(1, 3, True)
+        receptor(3, 3)

@@ -30,11 +30,11 @@ def tile_pair_tensor_messages_s8_kernel(
 ):
     nc = tc.nc
     left_v = left.rearrange("(g p t) d -> g p t d", p=P, t=4)
-    right_v = right.rearrange("(g p t) d -> g p t d", p=P, t=4)
+    right_v = right.rearrange("(g s q) d -> g q s d", s=4, q=P)
     prior_v = prior.rearrange("(g p t) m -> g p t m", p=P, t=4)
     near_v = near.rearrange("(g p t) m -> g p t m", p=P, t=4)
     lig_v = to_ligand.rearrange("(g p t) r -> g t p r", p=P, t=4)
-    rec_v = to_receptor.rearrange("(g p t) r -> g t p r", p=P, t=4)
+    rec_v = to_receptor.rearrange("(g s q) r -> g s q r", s=4, q=P)
 
     with ExitStack() as ctx:
         keep = ctx.enter_context(tc.tile_pool(name="keep", bufs=1))
@@ -146,31 +146,40 @@ def tile_pair_tensor_messages_s8_kernel(
                 )
             s1_banks[k, t] = bank
 
-        sums, zis, lis = {}, {}, {}
+        sums, zns, zis, lis, z_banks = {}, {}, {}, {}, {}
 
         def add_prior(k, t):
             g, b = ORDER[k]
             if t == 0:
                 sums[k] = work.tile([P, 4, 4 * P], F32, name="sum_t", tag="sum_t", bufs=2, align_bytes=64)
             nc.vector.tensor_tensor(
-                out=sums[k][:, t, :].rearrange("p (s q) -> p s q", s=4),
-                in0=s1_banks[k, t][:].rearrange("p (s q) -> p s q", s=4),
-                in1=priors[g, b][:, t, :].rearrange("p (q s) -> p s q", s=4),
-                op=ADD,
+                out=sums[k][:, t, :], in0=s1_banks[k, t][:], in1=priors[g, b][:, t, :], op=ADD
             )
 
-        def relu_near(k, s):
+        def relu_near(k, t0, t1):
             g, b = ORDER[k]
-            if s == 0:
-                zis[k] = work.tile([P, 4 * P, 4], BF16, name="zi", tag="zi", bufs=3, align_bytes=64)
+            if t0 == 0:
+                zns[k] = work.tile([P, 4, 4 * P], BF16, name="zn", tag="zn", bufs=3, align_bytes=64)
             nc.vector.scalar_tensor_tensor(
-                out=zis[k][:, P * s : P * (s + 1), :],
-                in0=sums[k][:, :, P * s : P * (s + 1)].rearrange("p t q -> p q t"),
+                out=zns[k][:, t0:t1].rearrange("p t m -> p (t m)"),
+                in0=sums[k][:, t0:t1].rearrange("p t m -> p (t m)"),
                 scalar=0.0,
-                in1=nears[g, b % 2][:].rearrange("p t (q s) -> p s q t", s=4)[:, s],
+                in1=nears[g, b % 2][:, t0:t1].rearrange("p t m -> p (t m)"),
                 op0=MAX,
                 op1=MULT,
             )
+
+        def group_a(k, c0, c1, engine):
+            if k not in zis:
+                zis[k] = work.tile([P, 4 * P, 4], BF16, name="zi", tag="zi", bufs=2, align_bytes=64)
+            dst = zis[k][:, P * c0 : P * c1, :].rearrange("p (c i) t -> p c t i", i=4)
+            src = zns[k][:, :, P * c0 : P * c1].rearrange("p t (c i) -> p c t i", i=4)
+            if engine == "v":
+                nc.vector.tensor_copy(out=dst, in_=src)
+            elif engine == "s":
+                nc.scalar.copy(out=dst, in_=src)
+            else:
+                nc.gpsimd.tensor_scalar(out=dst, in0=src, scalar1=1.0, scalar2=0.0, op0=MULT, op1=ADD)
 
         def quantize_a(k, s0=0, s1=4):
             g, b = ORDER[k]
@@ -180,31 +189,31 @@ def tile_pair_tensor_messages_s8_kernel(
                 in_=zis[k][:, P * s0 : P * s1].rearrange("p m t -> p (m t)"),
             )
 
-        z_banks = {}
+        def transpose_z(k, half):
+            bank = w_pool.tile([P, 2, 2, P], F32, name="bank", tag="bank", bufs=4)
+            z_banks[k, half] = bank
+            for tt in range(2):
+                words = zns[k][:, 2 * half + tt, :].bitcast(F32)
+                for u in range(2):
+                    nc.tensor.transpose(bank[:, tt, u, :], words[:, u : 2 * P : 2], ident[:])
 
-        def transpose_z(k, u, s0=0, s1=4):
-            words = zis[k][:].rearrange("p m t -> p (m t)").bitcast(F32)
-            if s0 == 0:
-                z_banks[k, u] = w_pool.tile([P, 4, P], F32, name="bank", tag="bank", bufs=4)
-            for s in range(s0, s1):
-                nc.tensor.transpose(z_banks[k, u][:, s, :], words[:, 256 * s + u : 256 * (s + 1) : 2], ident[:])
-
-        def copy_b(k, u, on_vector=False):
-            if u == 0:
-                lis[k] = work.tile([P, 2, 2, P, 4], BF16, name="li", tag="li", bufs=2, align_bytes=64)
-            dst = lis[k][:, u]
-            src = z_banks[k, u][:].rearrange("q s p -> q (s p)").bitcast(BF16).rearrange("q (s p e) -> q e p s", s=4, e=2)
+        def copy_b(k, half, on_vector=False):
+            if half == 0:
+                lis[k] = work.tile([P, 4, P, 4], BF16, name="li", tag="li", bufs=2, align_bytes=64)
+            dst = lis[k][:, 2 * half : 2 * half + 2].rearrange("q t p e -> q (t p e)").bitcast(F32)
+            dst = dst.rearrange("q (t p u) -> q t p u", t=2, u=2)
+            src = z_banks[k, half][:].rearrange("q t u p -> q t p u")
             if on_vector:
                 nc.vector.tensor_copy(out=dst, in_=src)
             else:
                 nc.scalar.copy(out=dst, in_=src)
 
-        def quantize_b(k, u0=0, u1=2):
+        def quantize_b(k, h0=0, h1=2):
             g, b = ORDER[k]
             nc.vector.quantize_mx(
-                out=zb_c[g, b][:, 2 * u0 : 2 * u1].rearrange("q t p -> q (t p)").bitcast(FP8X4),
-                scales=zb_s[g, b][:, 2 * u0 : 2 * u1].rearrange("q t p -> q (t p)"),
-                in_=lis[k][:, u0:u1].rearrange("q u e p s -> q (u e p s)"),
+                out=zb_c[g, b][:, 2 * h0 : 2 * h1].rearrange("q t p -> q (t p)").bitcast(FP8X4),
+                scales=zb_s[g, b][:, 2 * h0 : 2 * h1].rearrange("q t p -> q (t p)"),
+                in_=lis[k][:, 2 * h0 : 2 * h1].rearrange("q t p e -> q (t p e)"),
             )
 
         outs = {}
@@ -330,14 +339,12 @@ def tile_pair_tensor_messages_s8_kernel(
         widen_y(0)
         for t in range(4):
             rows(L1, t)
-        relu_near(0, 0)
-        relu_near(0, 1)
+        relu_near(0, 0, 2)
         quantize_left(1, 0, 2)
-        relu_near(0, 2)
+        relu_near(0, 2, 4)
         quantize_left(1, 2, 4)
         for t in range(4):
             stage1(1, t)
-        relu_near(0, 3)
         group_y(0)
         widen_y(1)
         for t in range(4):
@@ -380,9 +387,12 @@ def tile_pair_tensor_messages_s8_kernel(
         for k in range(1, N_UNITS):
             for t in range(4):
                 add_prior(k, t)
-            for u in range(2):
-                transpose_z(k - 1, u)
-                copy_b(k - 1, u)
+            group_a(k - 1, 0, 1, "g")
+            group_a(k - 1, 1, 2, "g")
+            for half in range(2):
+                transpose_z(k - 1, half)
+                copy_b(k - 1, half)
+            group_a(k - 1, 2, 4, "s")
             if k == 1:
                 load_v()
                 load_prior(0, 3)
@@ -396,27 +406,24 @@ def tile_pair_tensor_messages_s8_kernel(
             if k < last:
                 for t in range(4):
                     stage1(k + 1, t)
-            quantize_a(k - 1)
-            relu_near(k, 0)
-            relu_near(k, 1)
+            relu_near(k, 0, 2)
+            quantize_b(k - 1)
             if k == 1:
                 quantize_y(0)
                 group_y(1)
             if k == 2:
                 quantize_y(1)
+            quantize_a(k - 1)
             key = ahead.get(k)
             if key is not None:
                 for t in range(4):
                     rows(key, t)
             if k == 3:
-                receptor(0, 0)
-                receptor(0, 1)
-                receptor(0, 2)
-                receptor(0, 3)
+                for s in range(4):
+                    receptor(0, s)
             if k == 4:
                 for s in range(4):
                     receptor(1, s)
-            quantize_b(k - 1)
             if k == 5:
                 ligand_open(0, 0, False)
                 ligand_open(0, 1, False)
@@ -425,34 +432,34 @@ def tile_pair_tensor_messages_s8_kernel(
                 ligand_close(0, 1)
                 ligand(0, 2)
                 ligand(0, 3)
-            if k < last:
-                relu_near(k, 2)
-                relu_near(k, 3)
+            relu_near(k, 2, 4)
 
         for t in range(4):
             ligand_open(1, t, True)
-        for s in range(3):
-            receptor(2, s)
-        quantize_a(last, 0, 2)
-        relu_near(last, 2)
-        relu_near(last, 3)
-        for u in range(2):
-            transpose_z(last, u, 0, 2)
-        receptor(2, 3)
-        receptor(3, 0)
-        for u in range(2):
-            transpose_z(last, u, 2, 4)
+        receptor(2, 0)
+        transpose_z(last, 0)
+        copy_b(last, 0)
+        receptor(2, 1)
+        receptor(2, 2)
+        transpose_z(last, 1)
+        group_a(last, 0, 1, "v")
+        quantize_b(last, 0, 1)
+        group_a(last, 1, 2, "v")
+        quantize_a(last, 0, 1)
+        copy_b(last, 1)
+        group_a(last, 3, 4, "s")
         for t in range(4):
             ligand_passes(lig_banks[1, t], 1, t, [2])
-        copy_b(last, 0)
-        copy_b(last, 1, True)
-        quantize_a(last, 2, 4)
-        quantize_b(last, 0, 1)
+        receptor(2, 3)
+        group_a(last, 2, 3, "v")
+        quantize_a(last, 1, 2)
+        ligand_close(1, 0, True)
+        ligand_close(1, 1)
         quantize_b(last, 1, 2)
+        receptor(3, 0, True)
+        quantize_a(last, 2, 4)
         receptor(3, 1)
+        ligand_close(1, 2, True)
+        ligand_close(1, 3)
         receptor(3, 2, True)
-        ligand_close(1, 0)
-        ligand_close(1, 1, True)
-        ligand_close(1, 2)
-        ligand_close(1, 3, True)
         receptor(3, 3)

from contextlib import ExitStack

import concourse.mybir as mybir
from concourse.masks import make_identity

I, J, C, K, R = 1024, 1024, 2, 1024, 512
M = C * J
FLOPS = 2 * I * M * K + 2 * I * M * R + 2 * I * M * R

F32 = mybir.dt.float32
BF16 = mybir.dt.bfloat16
I32 = mybir.dt.int32
U32 = mybir.dt.uint32
U8 = mybir.dt.uint8
FP8 = mybir.dt.float8_e4m3fn
FP8X4 = mybir.dt.float8_e4m3fn_x4
FP4X4 = mybir.dt.float4_e2m1fn_x4
ADD = mybir.AluOpType.add
MAX = mybir.AluOpType.max
MULT = mybir.AluOpType.mult
COPY = mybir.ActivationFunctionType.Copy

P = 128
ORDER = [(0, 0), (1, 0), (0, 1), (1, 1), (0, 2), (0, 3), (1, 2), (1, 3)]
N_UNITS = len(ORDER)


def tile_pair_tensor_messages_s8_kernel(
    tc, left, right, prior, near, v_words, v_scales, y_bytes, y_scale, to_ligand, to_receptor
):
    nc = tc.nc
    left_v = left.rearrange("(g p t) d -> g p t d", p=P, t=4)
    right_v = right.rearrange("(g s q) d -> g q s d", s=4, q=P)
    prior_v = prior.rearrange("(g p t) m -> g p t m", p=P, t=4)
    near_v = near.rearrange("(g p t) m -> g p t m", p=P, t=4)
    lig_v = to_ligand.rearrange("(g p t) r -> g t p r", p=P, t=4)
    rec_v = to_receptor.rearrange("(g s q) r -> g s q r", s=4, q=P)

    with ExitStack() as ctx:
        keep = ctx.enter_context(tc.tile_pool(name="keep", bufs=1))
        work = ctx.enter_context(tc.tile_pool(name="work", bufs=2))
        s1_pool = ctx.enter_context(tc.psum_pool(name="s1", bufs=1))
        w_pool = ctx.enter_context(tc.psum_pool(name="w", bufs=4))
        ctx.enter_context(tc.manual_schedule())

        ident = keep.tile([P, P], F32, name="ident", align_bytes=64)
        make_identity(nc, ident[:])
        warm = keep.tile([P, 2], F32, name="warm", align_bytes=64)
        nc.gpsimd.memset(warm[:], 0.0)
        v_tile = keep.tile([P, 4, 2 * R], U8, name="v_tile", align_bytes=64)
        vs_tile = keep.tile([P, 4, R], U8, name="vs_tile", align_bytes=64)
        nc.gpsimd.memset(vs_tile[:].rearrange("p g n -> p (g n)").bitcast(I32), 0)
        nc.scalar.activation(warm[:, 1:2], warm[:, 0:1], COPY)

        lc = [keep.tile([P, 4, 2, P], U32, name=f"lc{g}", align_bytes=64) for g in range(2)]
        ls = [keep.tile([P, 4, 2, P], U8, name=f"ls{g}", align_bytes=64) for g in range(2)]
        rc = [keep.tile([P, 2, 4 * P], U32, name=f"rc{g}", align_bytes=64) for g in range(4)]
        rs = [keep.tile([P, 2, 4 * P], U8, name=f"rs{g}", align_bytes=64) for g in range(4)]
        yc = [keep.tile([P, R], U32, name=f"yc{g}", align_bytes=64) for g in range(2)]
        ys = [keep.tile([P, R], U8, name=f"ys{g}", align_bytes=64) for g in range(2)]
        za_c, za_s, zb_c, zb_s = {}, {}, {}, {}
        for g, b in ORDER:
            za_c[g, b] = keep.tile([P, 4 * P], U32, name=f"zac{g}{b}", align_bytes=64)
            za_s[g, b] = keep.tile([P, 4 * P], U8, name=f"zas{g}{b}", align_bytes=64)
            zb_c[g, b] = keep.tile([P, 4, P], U32, name=f"zbc{g}{b}", align_bytes=64)
            zb_s[g, b] = keep.tile([P, 4, P], U8, name=f"zbs{g}{b}", align_bytes=64)

        raws, priors, nears = {}, {}, {}

        def raw_tile(key):
            raw = work.tile([P, 4, K], BF16, name="raw", tag="raw", bufs=4, align_bytes=64)
            raws[key] = raw

        def load_raw(key, t0, t1):
            side, g = key
            view = left_v if side == "l" else right_v
            nc.sync.dma_start(out=raws[key][:, t0:t1, :], in_=view[g, :, t0:t1, :])

        def load_prior(g, b):
            t = work.tile([P, 4, 4 * P], BF16, name="prior_t", tag="prior_t", bufs=5, align_bytes=64)
            nc.sync.dma_start(out=t[:], in_=prior_v[g, :, :, 512 * b : 512 * (b + 1)])
            priors[g, b] = t

        def load_near(g, b):
            t = keep.tile([P, 4, 4 * P], BF16, name=f"near{g}{b}", align_bytes=64)
            nc.sync.dma_start(out=t[:], in_=near_v[g, :, :, 512 * b : 512 * (b + 1)])
            nears[g, b] = t

        def transpose_rows(key, t):
            words = raws[key][:].rearrange("p t d -> p (t d)").bitcast(F32)
            bank = w_pool.tile([P, 2, 2, P], F32, name="bank", tag="bank", bufs=4)
            for h in range(2):
                for u in range(2):
                    lo = 512 * t + 256 * h
                    nc.tensor.transpose(bank[:, h, u, :], words[:, lo + u : lo + 256 : 2], ident[:])
            return bank

        grouped = {}

        def copy_rows(key, t, bank, on_vector):
            side, g = key
            src = bank[:].rearrange("x h u p -> x h p u")
            if side == "l":
                if t == 0:
                    grouped[key] = work.tile([P, 4, 2, P, 4], BF16, name="rin", tag="rin", bufs=3, align_bytes=64)
                dst = grouped[key][:, t].rearrange("x h p e -> x (h p e)").bitcast(F32)
                dst = dst.rearrange("x (h p u) -> x h p u", h=2, u=2)
            else:
                if t == 0:
                    grouped[key] = work.tile([P, 2, 4, P, 4], BF16, name="rin", tag="rin", bufs=3, align_bytes=64)
                dst = grouped[key][:].rearrange("x h s p e -> x (h s p e)").bitcast(F32)
                dst = dst.rearrange("x (h s p u) -> x h s p u", h=2, s=4, u=2)[:, :, t]
            if on_vector:
                nc.vector.tensor_copy(out=dst, in_=src)
            else:
                nc.scalar.copy(out=dst, in_=src)

        def quantize_left(g, t0, t1):
            nc.vector.quantize_mx(
                out=lc[g][:, t0:t1].rearrange("x t h p -> x (t h p)").bitcast(FP8X4),
                scales=ls[g][:, t0:t1].rearrange("x t h p -> x (t h p)"),
                in_=grouped["l", g][:, t0:t1].rearrange("x t h p e -> x (t h p e)"),
            )

        def quantize_right(g, h, s0=0, s1=4):
            nc.vector.quantize_mx(
                out=rc[g][:, h, P * s0 : P * s1].bitcast(FP8X4),
                scales=rs[g][:, h, P * s0 : P * s1],
                in_=grouped["r", g][:, h, s0:s1].rearrange("x s p e -> x (s p e)"),
            )

        s1_banks = {}

        def stage1(k, t):
            g, b = ORDER[k]
            bank = s1_pool.tile([P, 4 * P], F32, name="s1b", tag=f"s1b{t}", bufs=1)
            for h in range(2):
                nc.tensor.matmul_mx(
                    out=bank[:],
                    lhsT=lc[g][:, t, h, :].bitcast(FP8X4),
                    lhsT_scale=ls[g][:, t, h, :],
                    rhs=rc[b][:, h, :].bitcast(FP8X4),
                    rhs_scale=rs[b][:, h, :],
                    start=(h == 0),
                    stop=(h == 1),
                )
            s1_banks[k, t] = bank

        sums, zns, zis, lis, z_banks = {}, {}, {}, {}, {}

        def add_prior(k, t):
            g, b = ORDER[k]
            if t == 0:
                sums[k] = work.tile([P, 4, 4 * P], F32, name="sum_t", tag="sum_t", bufs=2, align_bytes=64)
            nc.vector.tensor_tensor(
                out=sums[k][:, t, :], in0=s1_banks[k, t][:], in1=priors[g, b][:, t, :], op=ADD
            )

        def relu_near(k, t0, t1):
            g, b = ORDER[k]
            if t0 == 0:
                zns[k] = work.tile([P, 4, 4 * P], BF16, name="zn", tag="zn", bufs=3, align_bytes=64)
            nc.vector.scalar_tensor_tensor(
                out=zns[k][:, t0:t1].rearrange("p t m -> p (t m)"),
                in0=sums[k][:, t0:t1].rearrange("p t m -> p (t m)"),
                scalar=0.0,
                in1=nears[g, b % 2][:, t0:t1].rearrange("p t m -> p (t m)"),
                op0=MAX,
                op1=MULT,
            )

        def group_a(k, c0, c1, engine):
            if k not in zis:
                zis[k] = work.tile([P, 4 * P, 4], BF16, name="zi", tag="zi", bufs=2, align_bytes=64)
            dst = zis[k][:, P * c0 : P * c1, :].rearrange("p (c i) t -> p c t i", i=4)
            src = zns[k][:, :, P * c0 : P * c1].rearrange("p t (c i) -> p c t i", i=4)
            if engine == "v":
                nc.vector.tensor_copy(out=dst, in_=src)
            elif engine == "s":
                nc.scalar.copy(out=dst, in_=src)
            else:
                nc.gpsimd.tensor_scalar(out=dst, in0=src, scalar1=1.0, scalar2=0.0, op0=MULT, op1=ADD)

        def quantize_a(k, s0=0, s1=4):
            g, b = ORDER[k]
            nc.vector.quantize_mx(
                out=za_c[g, b][:, P * s0 : P * s1].bitcast(FP8X4),
                scales=za_s[g, b][:, P * s0 : P * s1],
                in_=zis[k][:, P * s0 : P * s1].rearrange("p m t -> p (m t)"),
            )

        def transpose_z(k, half):
            bank = w_pool.tile([P, 2, 2, P], F32, name="bank", tag="bank", bufs=4)
            z_banks[k, half] = bank
            for tt in range(2):
                words = zns[k][:, 2 * half + tt, :].bitcast(F32)
                for u in range(2):
                    nc.tensor.transpose(bank[:, tt, u, :], words[:, u : 2 * P : 2], ident[:])

        def copy_b(k, half, on_vector=False):
            if half == 0:
                lis[k] = work.tile([P, 4, P, 4], BF16, name="li", tag="li", bufs=2, align_bytes=64)
            dst = lis[k][:, 2 * half : 2 * half + 2].rearrange("q t p e -> q (t p e)").bitcast(F32)
            dst = dst.rearrange("q (t p u) -> q t p u", t=2, u=2)
            src = z_banks[k, half][:].rearrange("q t u p -> q t p u")
            if on_vector:
                nc.vector.tensor_copy(out=dst, in_=src)
            else:
                nc.scalar.copy(out=dst, in_=src)

        def quantize_b(k, h0=0, h1=2):
            g, b = ORDER[k]
            nc.vector.quantize_mx(
                out=zb_c[g, b][:, 2 * h0 : 2 * h1].rearrange("q t p -> q (t p)").bitcast(FP8X4),
                scales=zb_s[g, b][:, 2 * h0 : 2 * h1].rearrange("q t p -> q (t p)"),
                in_=lis[k][:, 2 * h0 : 2 * h1].rearrange("q t p e -> q (t p e)"),
            )

        outs = {}

        def finish(bank, kind, g, t, on_vector):
            if (kind, g) not in outs:
                outs[kind, g] = work.tile([P, 4, R], F32, name="raw", tag="raw", bufs=4, align_bytes=64)
            o = outs[kind, g][:, t, :]
            if on_vector:
                nc.vector.tensor_copy(out=o, in_=bank[:])
            else:
                nc.scalar.copy(out=o, in_=bank[:])
            nc.sync.dma_start(out=(rec_v if kind == "r" else lig_v)[g, t], in_=o)

        def receptor(b, s, on_vector=False):
            bank = w_pool.tile([P, R], F32, name="bank", tag="bank", bufs=4)
            for g in range(2):
                nc.tensor.matmul_mx(
                    out=bank[:],
                    lhsT=za_c[g, b][:, P * s : P * (s + 1)].bitcast(FP8X4),
                    lhsT_scale=za_s[g, b][:, P * s : P * (s + 1)],
                    rhs=yc[g][:].bitcast(FP8X4),
                    rhs_scale=ys[g][:],
                    start=(g == 0),
                    stop=(g == 1),
                )
            finish(bank, "r", b, s, on_vector)

        def ligand_passes(bank, g, t, blocks):
            for b in blocks:
                nc.tensor.matmul_mx(
                    out=bank[:],
                    lhsT=zb_c[g, b][:, t, :].bitcast(FP8X4),
                    lhsT_scale=zb_s[g, b][:, t, :],
                    rhs=v_tile[:, b, :].bitcast(FP4X4),
                    rhs_scale=vs_tile[:, b, :],
                    start=(b == 0),
                    stop=(b == 3),
                )

        def ligand(g, t, on_vector=False):
            bank = w_pool.tile([P, R], F32, name="bank", tag="bank", bufs=4)
            ligand_passes(bank, g, t, range(4))
            finish(bank, "l", g, t, on_vector)

        y_codes = keep.tile([P, 2, 4, R], U8, name="y_codes", align_bytes=64)
        y_sc = keep.tile([P, 2, 4], F32, name="y_sc", align_bytes=64)
        y_plane, y_group = {}, {}

        def load_y():
            nc.sync.dma_start(out=y_sc[:], in_=y_scale.rearrange("(g p t) o -> p g (t o)", p=P, t=4))
            nc.sync.dma_start(out=y_codes[:], in_=y_bytes.rearrange("(g p t) r -> p g t r", p=P, t=4))

        def widen_y(g):
            y_plane[g] = work.tile([P, 4, R], BF16, name="y_plane", tag="y_plane", bufs=2, align_bytes=64)
            for t in range(4):
                nc.scalar.activation(
                    y_plane[g][:, t, :], y_codes[:, g, t, :].bitcast(FP8), COPY, scale=y_sc[:, g, t : t + 1]
                )

        def group_y(g):
            y_group[g] = work.tile([P, R, 4], BF16, name="y_group", tag="y_group", bufs=1, align_bytes=64)
            nc.vector.tensor_copy(
                out=y_group[g][:].rearrange("p (c i) t -> p c t i", i=4),
                in_=y_plane[g][:].rearrange("p t (c i) -> p c t i", i=4),
            )

        def quantize_y(g):
            nc.vector.quantize_mx(
                out=yc[g][:].bitcast(FP8X4), scales=ys[g][:], in_=y_group[g][:].rearrange("p r t -> p (r t)")
            )

        L0, R0, L1, R1, R2, R3 = ("l", 0), ("r", 0), ("l", 1), ("r", 1), ("r", 2), ("r", 3)
        for key in (L0, R0, L1, R1):
            raw_tile(key)
        load_raw(L0, 0, 1)
        for s in range(4):
            load_raw(R0, s, s + 1)
        load_raw(L0, 1, 2)
        load_raw(L0, 2, 4)
        load_prior(0, 0)
        load_y()
        load_raw(L1, 0, 2)
        load_near(0, 0)
        load_raw(L1, 2, 4)
        load_prior(1, 0)
        load_near(1, 0)
        load_raw(R1, 0, 2)
        load_raw(R1, 2, 4)
        load_prior(0, 1)
        load_near(0, 1)
        load_prior(1, 1)
        load_near(1, 1)

        def rows(key, t, on_vector=False):
            bank = transpose_rows(key, t)
            copy_rows(key, t, bank, on_vector)

        rows(L0, 0, True)
        rows(R0, 0)
        rows(R0, 1, True)
        quantize_left(0, 0, 1)
        quantize_right(0, 0, 0, 1)
        quantize_right(0, 1, 0, 1)
        rows(R0, 2)
        rows(R0, 3, True)
        quantize_right(0, 0, 1, 3)
        quantize_right(0, 1, 1, 3)
        quantize_right(0, 0, 3, 4)
        quantize_right(0, 1, 3, 4)
        rows(L0, 1)
        stage1(0, 0)
        quantize_left(0, 1, 2)
        rows(L0, 2)
        rows(L0, 3)
        stage1(0, 1)
        add_prior(0, 0)
        quantize_left(0, 2, 4)
        stage1(0, 2)
        stage1(0, 3)
        for t in range(1, 4):
            add_prior(0, t)
        widen_y(0)
        for t in range(4):
            rows(L1, t)
        relu_near(0, 0, 2)
        quantize_left(1, 0, 2)
        relu_near(0, 2, 4)
        quantize_left(1, 2, 4)
        for t in range(4):
            stage1(1, t)
        group_y(0)
        widen_y(1)
        for t in range(4):
            rows(R1, t)

        raw_tile(R2)
        load_raw(R2, 0, 4)
        load_prior(0, 2)
        raw_tile(R3)
        load_raw(R3, 0, 4)

        def load_v():
            nc.sync.dma_start(
                out=v_tile[:].rearrange("p g n -> p (g n)").bitcast(I32).rearrange("p (g n) -> p g n", g=4),
                in_=v_words.bitcast(I32).rearrange("g p n -> p g n"),
            )
            vs_words = vs_tile[:].rearrange("p g n -> p (g n)").bitcast(I32).rearrange("p (g n) -> p g n", g=4)
            for quad in range(4):
                nc.sync.dma_start(
                    out=vs_words[32 * quad : 32 * quad + 4],
                    in_=v_scales.bitcast(I32)[:, 4 * quad : 4 * quad + 4, :].rearrange("g q n -> q g n"),
                )

        lig_banks = {}

        def ligand_open(g, t, pool_tag):
            if pool_tag:
                lig_banks[g, t] = s1_pool.tile([P, R], F32, name="s1b", tag=f"s1b{t}", bufs=1)
            else:
                lig_banks[g, t] = w_pool.tile([P, R], F32, name="bank", tag="bank", bufs=4)
            ligand_passes(lig_banks[g, t], g, t, range(2 if pool_tag else 3))

        def ligand_close(g, t, on_vector=False):
            ligand_passes(lig_banks[g, t], g, t, range(3, 4))
            finish(lig_banks[g, t], "l", g, t, on_vector)

        last = N_UNITS - 1
        ahead = {1: R2, 2: R3}
        fresh = {1: R1, 3: R2, 4: R3}
        for k in range(1, N_UNITS):
            for t in range(4):
                add_prior(k, t)
            group_a(k - 1, 0, 1, "g")
            group_a(k - 1, 1, 2, "g")
            for half in range(2):
                transpose_z(k - 1, half)
                copy_b(k - 1, half)
            group_a(k - 1, 2, 4, "s")
            if k == 1:
                load_v()
                load_prior(0, 3)
                load_prior(1, 2)
            if k == 2:
                load_prior(1, 3)
            key = fresh.get(k)
            if key is not None:
                quantize_right(key[1], 0)
                quantize_right(key[1], 1)
            if k < last:
                for t in range(4):
                    stage1(k + 1, t)
            relu_near(k, 0, 2)
            quantize_b(k - 1)
            if k == 1:
                quantize_y(0)
                group_y(1)
            if k == 2:
                quantize_y(1)
            quantize_a(k - 1)
            key = ahead.get(k)
            if key is not None:
                for t in range(4):
                    rows(key, t)
            if k == 3:
                for s in range(4):
                    receptor(0, s)
            if k == 4:
                for s in range(4):
                    receptor(1, s)
            if k == 5:
                ligand_open(0, 0, False)
                ligand_open(0, 1, False)
            if k == 6:
                ligand_close(0, 0)
                ligand_close(0, 1)
                ligand(0, 2)
                ligand(0, 3)
            relu_near(k, 2, 4)

        for t in range(4):
            ligand_open(1, t, True)
        receptor(2, 0)
        transpose_z(last, 0)
        copy_b(last, 0)
        receptor(2, 1)
        receptor(2, 2)
        transpose_z(last, 1)
        group_a(last, 0, 1, "v")
        quantize_b(last, 0, 1)
        group_a(last, 1, 2, "v")
        quantize_a(last, 0, 1)
        copy_b(last, 1)
        group_a(last, 3, 4, "s")
        for t in range(4):
            ligand_passes(lig_banks[1, t], 1, t, [2])
        receptor(2, 3)
        group_a(last, 2, 3, "v")
        quantize_a(last, 1, 2)
        ligand_close(1, 0, True)
        ligand_close(1, 1)
        quantize_b(last, 1, 2)
        receptor(3, 0, True)
        quantize_a(last, 2, 4)
        receptor(3, 1)
        ligand_close(1, 2, True)
        ligand_close(1, 3)
        receptor(3, 2, True)
        receptor(3, 3)
